import numpy as np, ml_dtypes
CORES = [16,32,48,64,80]
N = 5
import mx_ref
NC, G, MB = 256, 4, 2
C = np.float32(0.019)
BF = ml_dtypes.bfloat16
def cut(t, i, w=512):
    return t[:, w * i:w * i + w]
def tile(rs):
    return np.stack(rs, axis=2).reshape(128, -1).astype(BF)
def layer(w, X):
    out = []
    for i in range(G):
        for t in range(len(X)):
            p = mx_ref.matmul(mx_ref.quantize(cut(w, len(X) * i + t)), X[t])
            z = p if t == 0 else z + p
        out.append(z)
    return out
def act(Z):
    return [np.maximum(z, 0) * C for z in Z]
def masked(U, Z):
    return [(u * (z > 0)) * C for u, z in zip(U, Z)]
def setup_inputs(rng):
    def f(*shape):
        return mx_ref.flush((rng.standard_normal(shape, dtype=np.float32) * np.exp2(rng.integers(-2, 3, shape[:-1] + (1,)))).astype(BF))
    return {"x": f(N, 128, MB * 4 * NC), "e": f(N, 128, MB * 4 * NC), "w": f(N, 128, G * 512), "v": f(N, 128, G * 512)}
def setup_inputs_blocks(rng):
    d = setup_inputs(rng)
    for k in ("x", "e"): d[k] = mx_ref.spread(d[k], rng, 4)
    for k in ("w", "v"): d[k] = mx_ref.spread(d[k], rng, 1)
    return d
def setup_inputs_wide(rng):
    d = setup_inputs(rng)
    for k in ("x", "e"): d[k] = mx_ref.flush((d[k].astype(np.float32) * np.exp2(rng.integers(-8, 9, (N, 1, 1))).astype(np.float32)).astype(BF))
    return d
def setup_inputs_zeros(rng):
    d = setup_inputs(rng); v = d["x"].reshape(N, 128, -1, 4).copy()
    v[np.broadcast_to((rng.random((N, 1, v.shape[2], 1)) < 0.33), v.shape)] = 0
    d["x"] = v.reshape(d["x"].shape)
    return d
def reference(x, e, w, v):
    y = np.full((N, 128, MB * G * NC), np.nan, np.float32)
    for m in range(MB):
        a = mx_ref.quantize(cut(x[N - 1], m, 4 * NC)); Z = []
        for s in range(N):
            Z.append(layer(w[s], [a]))
            if s < N - 1: a = mx_ref.quantize(tile(act(Z[s])))
        b = mx_ref.quantize(cut(e[0], m, 4 * NC))
        for s in range(N - 1, 0, -1):
            b = mx_ref.quantize(tile(masked(layer(v[s], [b]), Z[s])))
        U = layer(v[0], [b])
        for i in range(G):
            y[0][:, NC * (G * m + i):NC * (G * m + i) + NC] = U[i] * (Z[0][i] > 0)
    return {"y": y}

from concourse.mybir import dt, AluOpType, ActivationFunctionType

RUNS = [(0, 128), (128, 256), (256, 384), (384, 512)]
R = len(RUNS)
COLS, NC, G = 512, 256, 4
QUARTER = COLS // 4
FACTOR = 0.019
F8, U8 = "float8_e4m3fn_x4", "uint8"

SCRATCH = {
    "xt": ("sbuf", [128, 4 * COLS], "bfloat16"),
    "et": ("sbuf", [128, 4 * COLS], "bfloat16"),
    "wt": ("sbuf", [128, G * 512], "bfloat16"),
    "vt": ("sbuf", [128, G * 512], "bfloat16"),
    "wq": ("sbuf", [128, COLS], F8), "ws": ("sbuf", [128, COLS], U8),
    "vq": ("sbuf", [128, COLS], F8), "vs": ("sbuf", [128, COLS], U8),
    "eq": ("sbuf", [128, COLS], F8), "es": ("sbuf", [128, COLS], U8),
    "ainq": ("sbuf", [128, COLS], F8), "ains": ("sbuf", [128, COLS], U8),
    "aoutq": ("sbuf", [128, COLS], F8), "aouts": ("sbuf", [128, COLS], U8),
    "binq": ("sbuf", [128, COLS], F8), "bins": ("sbuf", [128, COLS], U8),
    "boutq": ("sbuf", [128, COLS], F8), "bouts": ("sbuf", [128, COLS], U8),
    "ht": ("sbuf", [128, 4 * COLS], "bfloat16"),
    "bt": ("sbuf", [128, 4 * COLS], "bfloat16"),
    "fc": ("sbuf", [128, 4 * COLS], "float32"),
    "sg": ("sbuf", [128, 4 * COLS], "float32"),
    "fm": ("sbuf", [128, 4 * COLS], "bfloat16"),
    "ys": ("sbuf", [128, G * COLS], "float32"),
    "ps": ("psum", [128, 8 * 512], "float32"),
}
SEMAPHORES = (["lw", "lv", "wd", "vd", "um", "sent", "relay", "earr", "ysy", "ysc"]
              + ["le%d" % j for j in range(4)] + ["ed%d" % j for j in range(4)]
              + ["lx%d" % c for c in range(R)] + ["xd%d" % c for c in range(R)]
              + ["aarr%d" % c for c in range(R)] + ["barr%d" % c for c in range(R)]
              + ["mk%d" % c for c in range(R)] + ["sa%d" % c for c in range(R)]
              + ["q%d" % k for k in range(2 * R)] + ["t%d" % k for k in range(2 * R)]
              + ["m%d_%d" % (k, i) for k in range(2 * R) for i in range(G)]
              + ["p%d_%d" % (c, i) for c in range(R) for i in range(G)]
              + ["g%d_%d" % (c, i) for c in range(R) for i in (0, 2)])


def rank_program(g, core, T, topo):
    s = T.rank_of(core)
    if s is None:
        return
    S = T.sem
    last = len(T.cores) - 1
    vec, act, ten, syn = g.vector, g.scalar, g.tensor, g.sync
    MULT, MAX, GT = AluOpType.mult, AluOpType.max, AluOpType.is_gt
    RELU, SIGN = ActivationFunctionType.Relu, ActivationFunctionType.Sign
    sent = [0]

    def engines(src, dst):
        return bin(topo.mask(src, dst)).count("1")

    def send(dst_rank, out, in_, sem):
        dst = T.cores[dst_rank]
        rid, pid, _ = topo.addr(dst)
        g.remote_dma(out_ap=out, in_ap=in_, remote_sem=S[sem], local_sem=S["sent"], pid=pid, routing_id=rid,
                     dma_engine_mask=topo.mask(core, dst))
        sent[0] += engines(core, dst)

    def send_run(dst_rank, outq, outs, inq, ins, a, b, sem):
        send(dst_rank, T[outq][:, a:b].bitcast(dt.uint8), T[inq][:, a:b].bitcast(dt.uint8), sem)
        send(dst_rank, T[outs][:, a:b], T[ins][:, a:b], sem)

    def send_codes_of_e(dst_rank, j, sem):
        cols = slice(QUARTER * j, QUARTER * (j + 1))
        send(dst_rank, T.eq[:, cols].bitcast(dt.uint8), T.eq[:, cols].bitcast(dt.uint8), sem)

    def bank(j, n):
        return T.ps[:, 512 * j:512 * j + n]

    def quant_weights(src, q, sc, loaded, n, done):
        vec.wait_ge(S[loaded], n)
        for i in range(G):
            vec.quantize_mx(T[q][:, 128 * i:128 * i + 128], T[sc][:, 128 * i:128 * i + 128],
                            T[src][:, 512 * i:512 * i + 512]).then_inc(S[done], 1)

    def product(out, q, sc, i, mq, ms, a, b):
        return ten.matmul_mx(out, T[q][:, 128 * i:128 * i + 128], T[sc][:, 128 * i:128 * i + 128],
                             T[mq][:, a:b], T[ms][:, a:b], True, True)

    arrived = 2 * engines(T.cores[(s + 1) % len(T.cores)], core)

    if s == last:
        for c, (a, b) in enumerate(RUNS):
            (syn, act)[c % 2].dma_start(T.xt[:, 4 * a:4 * b], T.x[:, 4 * a:4 * b]).then_inc(S["lx%d" % c], 16)
        syn.dma_start(T.vt[:], T.v[:]).then_inc(S["lv"], 16)
        act.dma_start(T.wt[:], T.w[:]).then_inc(S["lw"], 16)
        for c, (a, b) in enumerate(RUNS):
            vec.wait_ge(S["lx%d" % c], 16)
            vec.quantize_mx(T.aoutq[:, a:b], T.aouts[:, a:b], T.xt[:, 4 * a:4 * b]).then_inc(S["xd%d" % c], 1)
            g.wait_ge(S["xd%d" % c], 1)
            send_run(0, "ainq", "ains", "aoutq", "aouts", a, b, "aarr%d" % c)
        quant_weights("vt", "vq", "vs", "lv", 16, "vd")
        quant_weights("wt", "wq", "ws", "lw", 16, "wd")
        ten.wait_ge(S["vd"], G)
        ten.wait_ge(S["earr"], sum(engines(T.cores[r], core) for r in (0, 0, 1, 2, 3)))
        for i in range(G):
            product(bank(i, COLS), "vq", "vs", i, "eq", "es", 0, COLS).then_inc(S["um"], 1)
        ten.wait_ge(S["wd"], G)
        vec.wait_ge(S["um"], G)
        for c, (a, b) in enumerate(RUNS):
            n = b - a
            ten.wait_ge(S["aarr%d" % c], arrived)
            for i in range(G):
                if c > 0:
                    ten.wait_ge(S["%s%d_%d" % ("g" if i in (0, 2) else "p", c - 1, i)], 1)
                product(bank(G + i, n), "wq", "ws", i, "ainq", "ains", a, b).then_inc(S["m%d_%d" % (c, i)], 1)

            def cols(i):
                return slice(4 * a + i, 4 * b, 4)
            for i in (0, 2):
                act.wait_ge(S["m%d_%d" % (c, i)], 1)
                act.activation(T.sg[:, cols(i)], bank(G + i, n), SIGN).then_inc(S["g%d_%d" % (c, i)], 1)
                act.wait_ge(S["g%d_%d" % (c, i)], 1)
                act.activation(T.fc[:, cols(i)], T.sg[:, cols(i)], RELU, scale=FACTOR).then_inc(S["p%d_%d" % (c, i)], 1)
            for i in (1, 0, 3, 2):
                if i in (1, 3):
                    vec.wait_ge(S["m%d_%d" % (c, i)], 1)
                    vec.tensor_scalar(T.fc[:, cols(i)], bank(G + i, n), 0.0, FACTOR, GT, MULT).then_inc(S["p%d_%d" % (c, i)], 1)
                vec.wait_ge(S["p%d_%d" % (c, i)], 1)
                vec.tensor_tensor(T.bt[:, cols(i)], T.ps[:, 512 * i + a:512 * i + b], T.fc[:, cols(i)], MULT).then_inc(S["t%d" % c], 1)
            vec.wait_ge(S["t%d" % c], G)
            vec.quantize_mx(T.boutq[:, a:b], T.bouts[:, a:b], T.bt[:, 4 * a:4 * b]).then_inc(S["q%d" % c], 1)
            g.wait_ge(S["q%d" % c], 1)
            send_run(s - 1, "binq", "bins", "boutq", "bouts", a, b, "barr%d" % c)
        g.wait_ge(S["sent"], sent[0])
        return

    if s == 0:
        def load_e(q, j):
            cols = slice(4 * QUARTER * j, 4 * QUARTER * (j + 1))
            q.dma_start(T.et[:, cols], T.e[:, cols]).then_inc(S["le%d" % j], 16)

        def quant_e(j):
            vec.wait_ge(S["le%d" % j], 16)
            vec.quantize_mx(T.eq[:, QUARTER * j:QUARTER * (j + 1)], T.es[:, QUARTER * j:QUARTER * (j + 1)],
                            T.et[:, 4 * QUARTER * j:4 * QUARTER * (j + 1)]).then_inc(S["ed%d" % j], 1)
        half = G * 512 // 2
        load_e(syn, 1)
        load_e(act, 2)
        load_e(syn, 3)
        act.dma_start(T.wt[:, :half], T.w[:, :half]).then_inc(S["lw"], 16)
        syn.dma_start(T.wt[:, half:], T.w[:, half:]).then_inc(S["lw"], 16)
        load_e(act, 0)
        syn.dma_start(T.vt[:], T.v[:]).then_inc(S["lv"], 16)
        for j in (1, 2, 3):
            quant_e(j)
            g.wait_ge(S["ed%d" % j], 1)
            send_codes_of_e(j, j, "relay")
        quant_weights("wt", "wq", "ws", "lw", 32, "wd")
        quant_e(0)
    else:
        syn.dma_start(T.wt[:], T.w[:]).then_inc(S["lw"], 16)
        act.dma_start(T.vt[:], T.v[:]).then_inc(S["lv"], 16)
        quant_weights("wt", "wq", "ws", "lw", 16, "wd")
        quant_weights("vt", "vq", "vs", "lv", 16, "vd")
        g.wait_ge(S["relay"], engines(T.cores[0], core))
        send_codes_of_e(last, s, "earr")

    ten.wait_ge(S["wd"], G)
    for k, (a, b) in enumerate(RUNS):
        n, base = b - a, G * (k % 2)

        def cols(i):
            return slice(4 * a + i, 4 * b, 4)
        ten.wait_ge(S["aarr%d" % k], arrived)
        if k >= 2:
            ten.wait_ge(S["q%d" % (k - 2)], 1)
        for i in range(G):
            product(bank(base + i, n), "wq", "ws", i, "ainq", "ains", a, b).then_inc(S["m%d_%d" % (k, i)], 1)
        for i in (0, 2):
            act.wait_ge(S["m%d_%d" % (k, i)], 1)
            act.activation(T.ht[:, cols(i)], bank(base + i, n), RELU, scale=FACTOR).then_inc(S["sa%d" % k], 1)
        for i in (1, 3):
            vec.wait_ge(S["m%d_%d" % (k, i)], 1)
            vec.tensor_scalar(T.ht[:, cols(i)], bank(base + i, n), 0.0, FACTOR, MAX, MULT).then_inc(S["t%d" % k], 1)
        vec.wait_ge(S["sa%d" % k], 2)
        vec.wait_ge(S["t%d" % k], 2)
        vec.quantize_mx(T.aoutq[:, a:b], T.aouts[:, a:b], T.ht[:, 4 * a:4 * b]).then_inc(S["q%d" % k], 1)
        if s == 0:
            vec.tensor_scalar(T.fm[:, 4 * a:4 * b], T.ht[:, 4 * a:4 * b], 0.0, None, GT).then_inc(S["mk%d" % k], 1)
        else:
            vec.tensor_scalar(T.fc[:, 4 * a:4 * b], T.ht[:, 4 * a:4 * b], 0.0, FACTOR, GT, MULT).then_inc(S["mk%d" % k], 1)
        g.wait_ge(S["q%d" % k], 1)
        send_run(s + 1, "ainq", "ains", "aoutq", "aouts", a, b, "aarr%d" % k)
    if s == 0:
        g.wait_ge(S["ed0"], 1)
        send_codes_of_e(last, 0, "earr")
        send(last, T.es[:], T.es[:], "earr")
        quant_weights("vt", "vq", "vs", "lv", 16, "vd")

    ten.wait_ge(S["vd"], G)
    stored = [0, 0]
    for c, (a, b) in enumerate(RUNS):
        k = R + c
        n, base = b - a, G * (k % 2)

        def cols(i):
            return slice(4 * a + i, 4 * b, 4)
        ten.wait_ge(S["barr%d" % c], arrived)
        for i in range(G):
            if s == 0 and c >= 2:
                ten.wait_ge(S["p%d_%d" % (c - 2, i)], 1)
            elif i == 0:
                ten.wait_ge(S["q%d" % (k - 2)], 1)
            product(bank(base + i, n), "vq", "vs", i, "binq", "bins", a, b).then_inc(S["m%d_%d" % (k, i)], 1)
        vec.wait_ge(S["mk%d" % c], 1)
        for i in range(G):
            vec.wait_ge(S["m%d_%d" % (k, i)], 1)
            if s > 0:
                vec.tensor_tensor(T.bt[:, cols(i)], bank(base + i, n), T.fc[:, cols(i)], MULT).then_inc(S["t%d" % k], 1)
                continue
            vec.tensor_tensor(T.ys[:, COLS * i + a:COLS * i + b], bank(base + i, n), T.fm[:, cols(i)],
                              MULT).then_inc(S["p%d_%d" % (c, i)], 1)
            q = (syn, act)[i % 2]
            q.wait_ge(S["p%d_%d" % (c, i)], 1)
            for m in range(COLS // NC):
                lo, hi = max(a, NC * m), min(b, NC * (m + 1))
                if lo < hi:
                    y0 = NC * (G * m + i) - NC * m
                    q.dma_start(T.y[:, y0 + lo:y0 + hi], T.ys[:, COLS * i + lo:COLS * i + hi]).then_inc(
                        S[("ysy", "ysc")[i % 2]], 16)
                    stored[i % 2] += 16
        if s > 0:
            vec.wait_ge(S["t%d" % k], G)
            vec.quantize_mx(T.boutq[:, a:b], T.bouts[:, a:b], T.bt[:, 4 * a:4 * b]).then_inc(S["q%d" % k], 1)
            g.wait_ge(S["q%d" % k], 1)
            send_run(s - 1, "binq", "bins", "boutq", "bouts", a, b, "barr%d" % c)
    if s == 0:
        syn.wait_ge(S["ysy"], stored[0])
        act.wait_ge(S["ysc"], stored[1])
    g.wait_ge(S["sent"], sent[0])
